import numpy as np
import ml_dtypes


def mxq(x, axis, fmt="e4m3"):
    dtype, down = {"e4m3": (ml_dtypes.float8_e4m3fn, 7), "e5m2": (ml_dtypes.float8_e5m2, 14)}[fmt]
    v = np.moveaxis(np.asarray(x, np.float32).astype(ml_dtypes.bfloat16).astype(np.float64), axis, -1)
    blocks = v.reshape(v.shape[:-1] + (-1, 32))
    amax = np.abs(blocks).max(-1, keepdims=True)
    byte = np.maximum(np.where(amax > 0, np.frexp(amax)[1] - 1 + 127, 0) - down, 1)
    scale = np.exp2(byte - 127.0)
    codes = (blocks / scale).astype(np.float32).astype(dtype).astype(np.float64)
    return np.moveaxis((codes * scale).reshape(v.shape), -1, axis)


WIDE = False


def mx_kscale(k):
    if not WIDE:
        return np.ones(k)
    levels = np.array([10, -10, 5, -5, 0])
    if k % 512:
        return np.exp2(np.random.permutation(np.resize(levels, k // 32))).repeat(32)
    a = np.empty((k // 512, 16))
    for p in range(k // 512):
        a[p, :8] = np.random.permutation(np.resize(levels, 8))
        for g in range(8):
            far = levels[np.abs(levels - a[p, g]) >= 10]
            a[p, g + 8] = far[np.random.randint(len(far))]
    return np.exp2(a.ravel()).repeat(32)


def f64(x):
    return np.asarray(x).astype(np.float64)


def striped(idx):
    return np.tile(idx.reshape(-1, 16).T, (8, 1)).astype(np.uint16)


def unstriped(offs):
    return offs[:16].T.reshape(-1).astype(np.int64)


def striped8(idx):
    return np.concatenate([x.reshape(-1, 16).T for x in idx]).astype(np.uint16)


def runs(offs, k):
    lists = np.stack([offs[16 * r : 16 * r + 16].T.reshape(-1) for r in range(8)]).astype(np.int64)
    return lists[np.arange(k) % 512 // 64]


def pack_weight(w):
    k, n = w.shape
    w = f64(np.asarray(w, np.float32).astype(ml_dtypes.bfloat16)).reshape(k // 32, 32, n)
    amax = np.abs(w).max(1)
    byte = np.clip(np.where(amax > 0, np.frexp(amax)[1] - 1 + 127 - 7, 1), 1, 254)
    scaled = (w * np.exp2(127.0 - byte)[:, None, :]).reshape(k, n).astype(np.float32)
    words = np.ascontiguousarray(scaled.reshape(k // 512, 128, 4, n).transpose(0, 1, 3, 2)).astype(ml_dtypes.float8_e4m3fn).view(np.uint8)
    return words, np.ascontiguousarray(byte.astype(np.uint8).reshape(k // 512, 16, n))


def unpack_weight(words, scales):
    g, p, n, _ = words.shape
    vals = np.ascontiguousarray(words).view(ml_dtypes.float8_e4m3fn).astype(np.float64) * np.repeat(np.exp2(scales.astype(np.float64) - 127.0), 8, axis=1)[..., None]
    return vals.transpose(0, 1, 3, 2).reshape(g * 512, n)


def relu(v):
    return np.maximum(v, 0.0)


K, T, S, V, N, G, H = 512, 2048, 512, 256, 512, 2048, 512


def setup_inputs():
    n = np.random.standard_normal
    s = mx_kscale(K)[:, None]
    u = mx_kscale(H)
    packed_xT = pack_weight(n((K, T)) * s)
    packed_dT = pack_weight(n((K, G)) / s)
    perm = np.stack([np.random.permutation(S) for _ in range(8)])
    return {
        "x_words": packed_xT[0],
        "x_scales": packed_xT[1],
        "d_words": packed_dT[0],
        "d_scales": packed_dT[1],
        "gn": (np.random.uniform(0.5, 1.5, (H, 1)) * u[:, None]).astype(np.float32),
        "w1": (n((H, N)) / np.sqrt(H) / u[:, None]).astype(np.float32),
        "offs": striped(np.random.permutation(T)[:S]),
        "kidx": striped8(np.random.randint(0, G, (8, H))),
        "la": striped8(perm[:, :V]),
        "lb": striped8(perm[:, V:]),
    }


def reference(x_words, x_scales, d_words, d_scales, gn, w1, offs, kidx, la, lb):
    d_kidx = unpack_weight(d_words, d_scales)[np.arange(K)[:, None], runs(kidx, K)]
    xq = unpack_weight(x_words, x_scales)[:, unstriped(offs)]
    s = 0.0625 * (d_kidx.T @ xq)
    b = s[np.arange(H)[:, None], runs(lb, H)]
    a = s[np.arange(H)[:, None], runs(la, H)]
    wb = relu(b - a)
    wa = relu(a - b)
    d1 = np.zeros((H, S))
    d1[np.arange(H)[:, None], runs(la, H)] = wa
    d2 = d1.copy()
    d2[np.arange(H)[:, None], runs(lb, H)] = wb
    z = f64(gn) * d2
    return mxq(f64(w1), 0, "e4m3").T @ mxq(z, 0, "e4m3")

@@ -1,0 +1,183 @@
+from contextlib import ExitStack
+
+import concourse.mybir as mybir
+
+K, T, S, V, N, G, H = 512, 2048, 512, 256, 512, 2048, 512
+FLOPS = 2 * K * H * S + 2 * H * N * S
+
+F32 = mybir.dt.float32
+BF16 = mybir.dt.bfloat16
+I32 = mybir.dt.int32
+U32 = mybir.dt.uint32
+U16 = mybir.dt.uint16
+U8 = mybir.dt.uint8
+FP8X4 = mybir.dt.float8_e4m3fn_x4
+ACT = mybir.ActivationFunctionType
+ALU = mybir.AluOpType
+
+P = 128
+PACK = 4
+HALF = S // 2
+SCORE_SCALE = 0.0625
+
+
+def tile_picked_scorefight_none_p_kernel(
+    tc, x_words, x_scales, d_words, d_scales, gn, w1, offs, kidx, la, lb, out
+):
+    nc = tc.nc
+    with ExitStack() as ctx:
+        lists = ctx.enter_context(tc.tile_pool(name="lists", bufs=1))
+        keep = ctx.enter_context(tc.tile_pool(name="keep", bufs=1))
+        psum = ctx.enter_context(tc.psum_pool(name="psum", bufs=1))
+
+        kidx_t = lists.tile([P, H // 16], U16, name="kidx_t")
+        offs_t = lists.tile([P, S // 16], U16, name="offs_t")
+        la_t = lists.tile([P, V // 16], U16, name="la_t")
+        lb_t = lists.tile([P, V // 16], U16, name="lb_t")
+
+        d_scale_table = keep.tile([P, G], U8, name="d_scale_table", align_bytes=64)
+        x_scale_table = keep.tile([P, T], U8, name="x_scale_table", align_bytes=64)
+        d_word_table = keep.tile([P, G], U32, name="d_word_table", align_bytes=64)
+        x_word_table = keep.tile([P, T], U32, name="x_word_table", align_bytes=64)
+        key_scales = keep.tile([P, H], U8, name="key_scales", align_bytes=64)
+        gain = keep.tile([P, PACK], F32, name="gain")
+
+        nc.vector.memset(d_scale_table[:].bitcast(I32), 0)
+        nc.vector.memset(x_scale_table[:].bitcast(I32), 0)
+        nc.gpsimd.memset(key_scales[:].bitcast(I32), 0)
+
+        nc.sync.dma_start(kidx_t[:], kidx)
+        nc.sync.dma_start(offs_t[:], offs)
+        nc.sync.dma_start(la_t[:], la)
+        nc.sync.dma_start(lb_t[:], lb)
+        nc.sync.dma_start(gain[:], gn.rearrange("(p t) o -> p (t o)", t=PACK))
+        nc.sync.dma_start(d_scale_table[0:P:8, :].bitcast(I32), d_scales[0].bitcast(I32))
+        nc.sync.dma_start(d_word_table[:].bitcast(I32), d_words[0].rearrange("p n t -> p (n t)").bitcast(I32))
+        for q in range(4):
+            nc.sync.dma_start(
+                x_scale_table[32 * q : 32 * q + 4, :].bitcast(I32), x_scales[0][4 * q : 4 * q + 4, :].bitcast(I32)
+            )
+        nc.sync.dma_start(x_word_table[:].bitcast(I32), x_words[0].rearrange("p n t -> p (n t)").bitcast(I32))
+
+        d_scales_picked = keep.tile([P, H], U8, name="d_scales_picked", align_bytes=64)
+        d_scales_dealt = keep.tile([P, H], U8, name="d_scales_dealt", tag="late", align_bytes=64)
+        nc.vector.tensor_copy(d_scales_picked[:], d_scale_table[:].indirect(kidx_t[:]))
+        nc.vector.tensor_copy(
+            d_scales_dealt[:].rearrange("p (t m) -> p t m", t=PACK),
+            d_scales_picked[:].rearrange("p (m t) -> p t m", t=PACK),
+        )
+        for c in range(4):
+            nc.scalar.dma_start(
+                key_scales[c:P:32, :].bitcast(I32),
+                d_scales_dealt[8 * c : P : 32, :].bitcast(I32),
+            )
+        w_raw = keep.tile([P, PACK, N], F32, name="w_raw", tag="late", align_bytes=64)
+        nc.sync.dma_start(w_raw[:], w1.rearrange("(p t) m -> p t m", t=PACK))
+
+        d_words_picked = keep.tile([P, H], U32, name="d_words_picked", align_bytes=64)
+        key_words = keep.tile([P, H], U32, name="key_words", align_bytes=64)
+        nc.vector.tensor_copy(d_words_picked[:], d_word_table[:].indirect(kidx_t[:]))
+        nc.vector.tensor_copy(
+            key_words[:].bitcast(I32).rearrange("p (t c i) -> p c t i", t=PACK, i=4),
+            d_words_picked[:].bitcast(I32).rearrange("p (c i t) -> p c t i", t=PACK, i=4),
+        )
+
+        query_scales = keep.tile([P, S], U8, name="query_scales", align_bytes=64)
+        query_words = keep.tile([P, S], U32, name="query_words", align_bytes=64)
+        nc.vector.tensor_copy(query_scales[:], x_scale_table[:].indirect(offs_t[:]))
+        for h in range(2):
+            nc.vector.tensor_copy(
+                query_words[:, h * HALF : (h + 1) * HALF],
+                x_word_table[:].indirect(offs_t[:, h * (HALF // 16) : (h + 1) * (HALF // 16)]),
+            )
+
+        banks = [psum.tile([P, S], F32, name="bank%d" % b) for b in range(8)]
+
+        def score(t, bank, cols):
+            keys = slice(t * P, (t + 1) * P)
+            nc.tensor.matmul_mx(
+                out=bank[:, cols],
+                lhsT=key_words[:, keys].bitcast(FP8X4),
+                lhsT_scale=key_scales[:, keys],
+                rhs=query_words[:, cols].bitcast(FP8X4),
+                rhs_scale=query_scales[:, cols],
+                start=True,
+                stop=True,
+            )
+
+        scores = [keep.tile([P, S], F32, name="scores%d" % t) for t in range(PACK)]
+        for h in range(2):
+            cols = slice(h * HALF, (h + 1) * HALF)
+            score(0, banks[h], cols)
+            nc.scalar.copy(scores[0][:, cols], banks[h][:, cols])
+        for t in range(1, PACK):
+            score(t, banks[t + 1], slice(0, S))
+            nc.scalar.copy(scores[t][:], banks[t + 1][:])
+
+        wins_a, wins_b = [], []
+        for t in range(PACK):
+            a = keep.tile([P, V], F32, name="a%d" % t)
+            lead = keep.tile([P, V], F32, name="lead%d" % t)
+            wa = keep.tile([P, V], F32, name="wa%d" % t)
+            wb = keep.tile([P, V], F32, name="wb%d" % t)
+            nc.vector.tensor_copy(a[:], scores[t][:].indirect(la_t[:]))
+            nc.vector.tensor_tensor(lead[:], scores[t][:].indirect(lb_t[:]), a[:], ALU.subtract)
+            nc.scalar.activation(wa[:], lead[:], ACT.Relu, scale=-SCORE_SCALE)
+            nc.scalar.activation(wb[:], lead[:], ACT.Relu, scale=SCORE_SCALE)
+            wins_a.append(wa)
+            wins_b.append(wb)
+
+        w_grouped = keep.tile([P, N, PACK], BF16, name="w_grouped", align_bytes=64)
+        w_words = keep.tile([P, N], U32, name="w_words", align_bytes=64)
+        w_scales = keep.tile([P, N], U8, name="w_scales", align_bytes=64)
+        for mt in range(N // P):
+            cols = slice(mt * P, (mt + 1) * P)
+            nc.scalar.copy(
+                w_grouped[:, cols, :].rearrange("p (c i) t -> p c t i", i=4),
+                w_raw[:, :, cols].rearrange("p t (c i) -> p c t i", i=4),
+            )
+        nc.vector.quantize_mx(
+            out=w_words[:].bitcast(FP8X4), scales=w_scales[:], in_=w_grouped[:].rearrange("p m t -> p (m t)")
+        )
+
+        z_grouped = [keep.tile([P, HALF, PACK], BF16, name="z_grouped%d" % h, align_bytes=64) for h in range(2)]
+        placed = [keep.tile([P, S], F32, name="placed%d" % t) for t in range(PACK)]
+        for t in range(PACK):
+            nc.vector.tensor_copy(placed[t][:].indirect(la_t[:]), wins_a[t][:])
+            nc.vector.tensor_copy(placed[t][:].indirect(lb_t[:]), wins_b[t][:])
+            for h in range(2):
+                cols = slice(h * HALF, (h + 1) * HALF)
+                if t >= PACK - 2 and h == 0:
+                    nc.vector.tensor_scalar(
+                        z_grouped[h][:, :, t], placed[t][:, cols], gain[:, t : t + 1], None, ALU.mult
+                    )
+                else:
+                    nc.scalar.activation(
+                        z_grouped[h][:, :, t], placed[t][:, cols], ACT.Copy, scale=gain[:, t : t + 1]
+                    )
+
+        for h in range(2):
+            cols = slice(h * HALF, (h + 1) * HALF)
+            z_words = keep.tile([P, HALF], U32, name="z_words%d" % h, align_bytes=64)
+            z_scales = keep.tile([P, HALF], U8, name="z_scales%d" % h, align_bytes=64)
+            nc.vector.quantize_mx(
+                out=z_words[:].bitcast(FP8X4), scales=z_scales[:], in_=z_grouped[h][:].rearrange("p j t -> p (j t)")
+            )
+            for mt in range(N // P):
+                bank = banks[4 * h + mt]
+                rows = slice(mt * P, (mt + 1) * P)
+                nc.tensor.matmul_mx(
+                    out=bank[:, 0:HALF],
+                    lhsT=w_words[:, rows].bitcast(FP8X4),
+                    lhsT_scale=w_scales[:, rows],
+                    rhs=z_words[:].bitcast(FP8X4),
+                    rhs_scale=z_scales[:],
+                    start=True,
+                    stop=True,
+                )
+                result = keep.tile([P, HALF], F32, name="result%d_%d" % (h, mt))
+                if mt % 2 == 0:
+                    nc.scalar.copy(result[:], bank[:, 0:HALF])
+                else:
+                    nc.vector.tensor_copy(result[:], bank[:, 0:HALF])
+                nc.sync.dma_start(out[rows, cols], result[:])

@@ -19,6 +19,7 @@ P = 128
 PACK = 4
 HALF = S // 2
 SCORE_SCALE = 0.0625
+ORDER = (2, 0, 1, 3)
 
 
 def tile_picked_scorefight_none_p_kernel(
@@ -36,11 +37,12 @@ def tile_picked_scorefight_none_p_kernel(
         lb_t = lists.tile([P, V // 16], U16, name="lb_t")
 
         d_scale_table = keep.tile([P, G], U8, name="d_scale_table", align_bytes=64)
-        x_scale_table = keep.tile([P, T], U8, name="x_scale_table", align_bytes=64)
+        x_scale_table = keep.tile([P, T], U8, name="x_scale_table", tag="x_order", align_bytes=64)
         d_word_table = keep.tile([P, G], U32, name="d_word_table", align_bytes=64)
         x_word_table = keep.tile([P, T], U32, name="x_word_table", align_bytes=64)
         key_scales = keep.tile([P, H], U8, name="key_scales", align_bytes=64)
         gain = keep.tile([P, PACK], F32, name="gain")
+        gain_raw = keep.tile([P, PACK], F32, name="gain_raw")
 
         nc.vector.memset(d_scale_table[:].bitcast(I32), 0)
         nc.vector.memset(x_scale_table[:].bitcast(I32), 0)
@@ -48,18 +50,19 @@ def tile_picked_scorefight_none_p_kernel(
 
         nc.sync.dma_start(kidx_t[:], kidx)
         nc.sync.dma_start(offs_t[:], offs)
-        nc.sync.dma_start(la_t[:], la)
-        nc.sync.dma_start(lb_t[:], lb)
-        nc.sync.dma_start(gain[:], gn.rearrange("(p t) o -> p (t o)", t=PACK))
+        nc.scalar.dma_start(d_word_table[:].bitcast(I32), d_words[0].rearrange("p n t -> p (n t)").bitcast(I32))
+        nc.scalar.dma_start(x_word_table[:].bitcast(I32), x_words[0].rearrange("p n t -> p (n t)").bitcast(I32))
         nc.sync.dma_start(d_scale_table[0:P:8, :].bitcast(I32), d_scales[0].bitcast(I32))
-        nc.sync.dma_start(d_word_table[:].bitcast(I32), d_words[0].rearrange("p n t -> p (n t)").bitcast(I32))
         for q in range(4):
             nc.sync.dma_start(
                 x_scale_table[32 * q : 32 * q + 4, :].bitcast(I32), x_scales[0][4 * q : 4 * q + 4, :].bitcast(I32)
             )
-        nc.sync.dma_start(x_word_table[:].bitcast(I32), x_words[0].rearrange("p n t -> p (n t)").bitcast(I32))
+        nc.sync.dma_start(gain_raw[:], gn.rearrange("(p t) o -> p (t o)", t=PACK))
+        nc.sync.dma_start(la_t[:], la)
+        nc.sync.dma_start(lb_t[:], lb)
+        nc.scalar.activation(gain[:], gain_raw[:], ACT.Copy, scale=SCORE_SCALE)
 
-        d_scales_picked = keep.tile([P, H], U8, name="d_scales_picked", align_bytes=64)
+        d_scales_picked = keep.tile([P, H], U8, name="d_scales_picked", tag="picked", align_bytes=64)
         d_scales_dealt = keep.tile([P, H], U8, name="d_scales_dealt", tag="late", align_bytes=64)
         nc.vector.tensor_copy(d_scales_picked[:], d_scale_table[:].indirect(kidx_t[:]))
         nc.vector.tensor_copy(
@@ -67,14 +70,14 @@ def tile_picked_scorefight_none_p_kernel(
             d_scales_picked[:].rearrange("p (m t) -> p t m", t=PACK),
         )
         for c in range(4):
-            nc.scalar.dma_start(
+            nc.sync.dma_start(
                 key_scales[c:P:32, :].bitcast(I32),
                 d_scales_dealt[8 * c : P : 32, :].bitcast(I32),
             )
         w_raw = keep.tile([P, PACK, N], F32, name="w_raw", tag="late", align_bytes=64)
         nc.sync.dma_start(w_raw[:], w1.rearrange("(p t) m -> p t m", t=PACK))
 
-        d_words_picked = keep.tile([P, H], U32, name="d_words_picked", align_bytes=64)
+        d_words_picked = keep.tile([P, H], U32, name="d_words_picked", tag="picked", align_bytes=64)
         key_words = keep.tile([P, H], U32, name="key_words", align_bytes=64)
         nc.vector.tensor_copy(d_words_picked[:], d_word_table[:].indirect(kidx_t[:]))
         nc.vector.tensor_copy(
@@ -83,7 +86,7 @@ def tile_picked_scorefight_none_p_kernel(
         )
 
         query_scales = keep.tile([P, S], U8, name="query_scales", align_bytes=64)
-        query_words = keep.tile([P, S], U32, name="query_words", align_bytes=64)
+        query_words = keep.tile([P, S], U32, name="query_words", tag="x_order", align_bytes=64)
         nc.vector.tensor_copy(query_scales[:], x_scale_table[:].indirect(offs_t[:]))
         for h in range(2):
             nc.vector.tensor_copy(
@@ -108,24 +111,28 @@ def tile_picked_scorefight_none_p_kernel(
         scores = [keep.tile([P, S], F32, name="scores%d" % t) for t in range(PACK)]
         for h in range(2):
             cols = slice(h * HALF, (h + 1) * HALF)
-            score(0, banks[h], cols)
-            nc.scalar.copy(scores[0][:, cols], banks[h][:, cols])
-        for t in range(1, PACK):
-            score(t, banks[t + 1], slice(0, S))
-            nc.scalar.copy(scores[t][:], banks[t + 1][:])
+            score(ORDER[0], banks[h], cols)
+            nc.scalar.copy(scores[ORDER[0]][:, cols], banks[h][:, cols])
+        for n, t in enumerate(ORDER[1:]):
+            score(t, banks[n + 2], slice(0, S))
+            nc.scalar.copy(scores[t][:], banks[n + 2][:])
 
-        wins_a, wins_b = [], []
-        for t in range(PACK):
-            a = keep.tile([P, V], F32, name="a%d" % t)
-            lead = keep.tile([P, V], F32, name="lead%d" % t)
-            wa = keep.tile([P, V], F32, name="wa%d" % t)
+        leads, wins = {}, {}
+
+        def fight(t, tag):
+            wa = keep.tile([P, V], F32, name="wa%d" % t, tag=tag)
             wb = keep.tile([P, V], F32, name="wb%d" % t)
+            nc.scalar.activation(wa[:], leads[t][:], ACT.Relu, scale=-1.0)
+            nc.scalar.activation(wb[:], leads[t][:], ACT.Relu)
+            wins[t] = (wa, wb)
+
+        for t in ORDER:
+            a = keep.tile([P, V], F32, name="a%d" % t)
+            leads[t] = keep.tile([P, V], F32, name="lead%d" % t)
             nc.vector.tensor_copy(a[:], scores[t][:].indirect(la_t[:]))
-            nc.vector.tensor_tensor(lead[:], scores[t][:].indirect(lb_t[:]), a[:], ALU.subtract)
-            nc.scalar.activation(wa[:], lead[:], ACT.Relu, scale=-SCORE_SCALE)
-            nc.scalar.activation(wb[:], lead[:], ACT.Relu, scale=SCORE_SCALE)
-            wins_a.append(wa)
-            wins_b.append(wb)
+            nc.vector.tensor_tensor(leads[t][:], scores[t][:].indirect(lb_t[:]), a[:], ALU.subtract)
+            if t != ORDER[-1]:
+                fight(t, "wa%d" % t)
 
         w_grouped = keep.tile([P, N, PACK], BF16, name="w_grouped", align_bytes=64)
         w_words = keep.tile([P, N], U32, name="w_words", align_bytes=64)
@@ -141,20 +148,20 @@ def tile_picked_scorefight_none_p_kernel(
         )
 
         z_grouped = [keep.tile([P, HALF, PACK], BF16, name="z_grouped%d" % h, align_bytes=64) for h in range(2)]
-        placed = [keep.tile([P, S], F32, name="placed%d" % t) for t in range(PACK)]
-        for t in range(PACK):
-            nc.vector.tensor_copy(placed[t][:].indirect(la_t[:]), wins_a[t][:])
-            nc.vector.tensor_copy(placed[t][:].indirect(lb_t[:]), wins_b[t][:])
+        for t in ORDER:
+            last = t == ORDER[-1]
+            wa, wb = wins[t]
+            placed = keep.tile([P, S], F32, name="placed%d" % t, tag="placed%d" % t)
+            nc.vector.tensor_copy(placed[:].indirect(la_t[:]), wa[:])
+            nc.vector.tensor_copy(placed[:].indirect(lb_t[:]), wb[:])
             for h in range(2):
                 cols = slice(h * HALF, (h + 1) * HALF)
-                if t >= PACK - 2 and h == 0:
-                    nc.vector.tensor_scalar(
-                        z_grouped[h][:, :, t], placed[t][:, cols], gain[:, t : t + 1], None, ALU.mult
-                    )
+                if last and h == 0:
+                    nc.vector.tensor_scalar(z_grouped[h][:, :, t], placed[:, cols], gain[:, t : t + 1], None, ALU.mult)
                 else:
-                    nc.scalar.activation(
-                        z_grouped[h][:, :, t], placed[t][:, cols], ACT.Copy, scale=gain[:, t : t + 1]
-                    )
+                    nc.scalar.activation(z_grouped[h][:, :, t], placed[:, cols], ACT.Copy, scale=gain[:, t : t + 1])
+            if t == ORDER[0]:
+                fight(ORDER[-1], "placed%d" % t)
 
         for h in range(2):
             cols = slice(h * HALF, (h + 1) * HALF)

@@ -20,6 +20,8 @@ PACK = 4
 HALF = S // 2
 SCORE_SCALE = 0.0625
 ORDER = (2, 0, 1, 3)
+EARLY = 256
+QUARTER = HALF // 2
 
 
 def tile_picked_scorefight_none_p_kernel(
@@ -37,47 +39,47 @@ def tile_picked_scorefight_none_p_kernel(
         lb_t = lists.tile([P, V // 16], U16, name="lb_t")
 
         d_scale_table = keep.tile([P, G], U8, name="d_scale_table", align_bytes=64)
-        x_scale_table = keep.tile([P, T], U8, name="x_scale_table", tag="x_order", align_bytes=64)
+        x_scale_table = keep.tile([P, T], U8, name="x_scale_table", align_bytes=64)
         d_word_table = keep.tile([P, G], U32, name="d_word_table", align_bytes=64)
-        x_word_table = keep.tile([P, T], U32, name="x_word_table", align_bytes=64)
-        key_scales = keep.tile([P, H], U8, name="key_scales", align_bytes=64)
+        x_word_table = keep.tile([P, T], U32, name="x_word_table", tag="late", align_bytes=64)
         gain = keep.tile([P, PACK], F32, name="gain")
         gain_raw = keep.tile([P, PACK], F32, name="gain_raw")
 
-        nc.vector.memset(d_scale_table[:].bitcast(I32), 0)
         nc.vector.memset(x_scale_table[:].bitcast(I32), 0)
-        nc.gpsimd.memset(key_scales[:].bitcast(I32), 0)
+        nc.vector.memset(d_scale_table[:].bitcast(I32), 0)
 
-        nc.sync.dma_start(kidx_t[:], kidx)
         nc.sync.dma_start(offs_t[:], offs)
-        nc.scalar.dma_start(d_word_table[:].bitcast(I32), d_words[0].rearrange("p n t -> p (n t)").bitcast(I32))
-        nc.scalar.dma_start(x_word_table[:].bitcast(I32), x_words[0].rearrange("p n t -> p (n t)").bitcast(I32))
+        nc.sync.dma_start(kidx_t[:], kidx)
+        d_words_i32 = d_words[0].rearrange("p n t -> p (n t)").bitcast(I32)
+        nc.sync.dma_start(d_word_table[:, 0:EARLY].bitcast(I32), d_words_i32[:, 0:EARLY])
+        nc.sync.dma_start(x_scale_table[0:P:8, :].bitcast(I32), x_scales[0].bitcast(I32))
         nc.sync.dma_start(d_scale_table[0:P:8, :].bitcast(I32), d_scales[0].bitcast(I32))
-        for q in range(4):
-            nc.sync.dma_start(
-                x_scale_table[32 * q : 32 * q + 4, :].bitcast(I32), x_scales[0][4 * q : 4 * q + 4, :].bitcast(I32)
-            )
+        nc.sync.dma_start(d_word_table[:, EARLY:G].bitcast(I32), d_words_i32[:, EARLY:G])
         nc.sync.dma_start(gain_raw[:], gn.rearrange("(p t) o -> p (t o)", t=PACK))
         nc.sync.dma_start(la_t[:], la)
         nc.sync.dma_start(lb_t[:], lb)
+        nc.sync.dma_start(x_word_table[:].bitcast(I32), x_words[0].rearrange("p n t -> p (n t)").bitcast(I32))
         nc.scalar.activation(gain[:], gain_raw[:], ACT.Copy, scale=SCORE_SCALE)
 
-        d_scales_picked = keep.tile([P, H], U8, name="d_scales_picked", tag="picked", align_bytes=64)
-        d_scales_dealt = keep.tile([P, H], U8, name="d_scales_dealt", tag="late", align_bytes=64)
-        nc.vector.tensor_copy(d_scales_picked[:], d_scale_table[:].indirect(kidx_t[:]))
-        nc.vector.tensor_copy(
-            d_scales_dealt[:].rearrange("p (t m) -> p t m", t=PACK),
-            d_scales_picked[:].rearrange("p (m t) -> p t m", t=PACK),
-        )
+        d_scales_picked = keep.tile([P, H], U8, name="d_scales_picked", align_bytes=64)
+        x_scales_picked = keep.tile([P, S], U8, name="x_scales_picked", align_bytes=64)
+        key_scales = keep.tile([P, H], U8, name="key_scales", align_bytes=64)
+        query_scales = keep.tile([P, S], U8, name="query_scales", align_bytes=64)
+        nc.vector.memset(query_scales[:].bitcast(I32), 0)
+        nc.vector.tensor_copy(x_scales_picked[:], x_scale_table[:].indirect(offs_t[:]))
         for c in range(4):
             nc.sync.dma_start(
-                key_scales[c:P:32, :].bitcast(I32),
-                d_scales_dealt[8 * c : P : 32, :].bitcast(I32),
+                query_scales[c:P:32, :].bitcast(I32), x_scales_picked[8 * c : P : 32, :].bitcast(I32)
             )
-        w_raw = keep.tile([P, PACK, N], F32, name="w_raw", tag="late", align_bytes=64)
-        nc.sync.dma_start(w_raw[:], w1.rearrange("(p t) m -> p t m", t=PACK))
+        nc.vector.tensor_copy(d_scales_picked[:], d_scale_table[:].indirect(kidx_t[:]))
+        nc.vector.tensor_copy(
+            key_scales[:].rearrange("p (t m) -> p t m", t=PACK),
+            d_scales_picked[:].rearrange("p (m t) -> p t m", t=PACK),
+        )
+        for c in range(1, 4):
+            nc.sync.dma_start(key_scales[c:P:32, :].bitcast(I32), key_scales[8 * c : P : 32, :].bitcast(I32))
 
-        d_words_picked = keep.tile([P, H], U32, name="d_words_picked", tag="picked", align_bytes=64)
+        d_words_picked = keep.tile([P, H], U32, name="d_words_picked", align_bytes=64)
         key_words = keep.tile([P, H], U32, name="key_words", align_bytes=64)
         nc.vector.tensor_copy(d_words_picked[:], d_word_table[:].indirect(kidx_t[:]))
         nc.vector.tensor_copy(
@@ -85,14 +87,15 @@ def tile_picked_scorefight_none_p_kernel(
             d_words_picked[:].bitcast(I32).rearrange("p (c i t) -> p c t i", t=PACK, i=4),
         )
 
-        query_scales = keep.tile([P, S], U8, name="query_scales", align_bytes=64)
-        query_words = keep.tile([P, S], U32, name="query_words", tag="x_order", align_bytes=64)
-        nc.vector.tensor_copy(query_scales[:], x_scale_table[:].indirect(offs_t[:]))
+        query_words = keep.tile([P, S], U32, name="query_words", align_bytes=64)
         for h in range(2):
             nc.vector.tensor_copy(
                 query_words[:, h * HALF : (h + 1) * HALF],
                 x_word_table[:].indirect(offs_t[:, h * (HALF // 16) : (h + 1) * (HALF // 16)]),
             )
+
+        w_raw = keep.tile([P, PACK, N], F32, name="w_raw", tag="late", align_bytes=64)
+        nc.sync.dma_start(w_raw[:], w1.rearrange("(p t) m -> p t m", t=PACK))
 
         banks = [psum.tile([P, S], F32, name="bank%d" % b) for b in range(8)]
 
@@ -157,34 +160,41 @@ def tile_picked_scorefight_none_p_kernel(
             for h in range(2):
                 cols = slice(h * HALF, (h + 1) * HALF)
                 if last and h == 0:
-                    nc.vector.tensor_scalar(z_grouped[h][:, :, t], placed[:, cols], gain[:, t : t + 1], None, ALU.mult)
+                    for u in range(2):
+                        part = slice(u * QUARTER, (u + 1) * QUARTER)
+                        nc.vector.tensor_scalar(
+                            z_grouped[h][:, part, t], placed[:, part], gain[:, t : t + 1], None, ALU.mult
+                        )
                 else:
                     nc.scalar.activation(z_grouped[h][:, :, t], placed[:, cols], ACT.Copy, scale=gain[:, t : t + 1])
             if t == ORDER[0]:
                 fight(ORDER[-1], "placed%d" % t)
 
-        for h in range(2):
-            cols = slice(h * HALF, (h + 1) * HALF)
+        for h, parts in enumerate(([slice(0, QUARTER), slice(QUARTER, HALF)], [slice(0, HALF)])):
             z_words = keep.tile([P, HALF], U32, name="z_words%d" % h, align_bytes=64)
             z_scales = keep.tile([P, HALF], U8, name="z_scales%d" % h, align_bytes=64)
-            nc.vector.quantize_mx(
-                out=z_words[:].bitcast(FP8X4), scales=z_scales[:], in_=z_grouped[h][:].rearrange("p j t -> p (j t)")
-            )
+            for part in parts:
+                nc.vector.quantize_mx(
+                    out=z_words[:, part].bitcast(FP8X4),
+                    scales=z_scales[:, part],
+                    in_=z_grouped[h][:, part, :].rearrange("p j t -> p (j t)"),
+                )
             for mt in range(N // P):
                 bank = banks[4 * h + mt]
                 rows = slice(mt * P, (mt + 1) * P)
-                nc.tensor.matmul_mx(
-                    out=bank[:, 0:HALF],
-                    lhsT=w_words[:, rows].bitcast(FP8X4),
-                    lhsT_scale=w_scales[:, rows],
-                    rhs=z_words[:].bitcast(FP8X4),
-                    rhs_scale=z_scales[:],
-                    start=True,
-                    stop=True,
-                )
+                for part in parts:
+                    nc.tensor.matmul_mx(
+                        out=bank[:, part],
+                        lhsT=w_words[:, rows].bitcast(FP8X4),
+                        lhsT_scale=w_scales[:, rows],
+                        rhs=z_words[:, part].bitcast(FP8X4),
+                        rhs_scale=z_scales[:, part],
+                        start=True,
+                        stop=True,
+                    )
                 result = keep.tile([P, HALF], F32, name="result%d_%d" % (h, mt))
                 if mt % 2 == 0:
                     nc.scalar.copy(result[:], bank[:, 0:HALF])
                 else:
                     nc.vector.tensor_copy(result[:], bank[:, 0:HALF])
-                nc.sync.dma_start(out[rows, cols], result[:])
+                nc.sync.dma_start(out[rows, h * HALF : (h + 1) * HALF], result[:])

@@ -20,7 +20,7 @@ PACK = 4
 HALF = S // 2
 SCORE_SCALE = 0.0625
 ORDER = (2, 0, 1, 3)
-EARLY = 256
+EARLY = 512
 QUARTER = HALF // 2
 
 
@@ -41,17 +41,17 @@ def tile_picked_scorefight_none_p_kernel(
         d_scale_table = keep.tile([P, G], U8, name="d_scale_table", align_bytes=64)
         x_scale_table = keep.tile([P, T], U8, name="x_scale_table", align_bytes=64)
         d_word_table = keep.tile([P, G], U32, name="d_word_table", align_bytes=64)
-        x_word_table = keep.tile([P, T], U32, name="x_word_table", tag="late", align_bytes=64)
+        x_word_table = keep.tile([P, T], U32, name="x_word_table", align_bytes=64)
         gain = keep.tile([P, PACK], F32, name="gain")
         gain_raw = keep.tile([P, PACK], F32, name="gain_raw")
 
         nc.vector.memset(x_scale_table[:].bitcast(I32), 0)
         nc.vector.memset(d_scale_table[:].bitcast(I32), 0)
 
-        nc.sync.dma_start(offs_t[:], offs)
-        nc.sync.dma_start(kidx_t[:], kidx)
         d_words_i32 = d_words[0].rearrange("p n t -> p (n t)").bitcast(I32)
         nc.sync.dma_start(d_word_table[:, 0:EARLY].bitcast(I32), d_words_i32[:, 0:EARLY])
+        nc.sync.dma_start(offs_t[:], offs)
+        nc.sync.dma_start(kidx_t[:], kidx)
         nc.sync.dma_start(x_scale_table[0:P:8, :].bitcast(I32), x_scales[0].bitcast(I32))
         nc.sync.dma_start(d_scale_table[0:P:8, :].bitcast(I32), d_scales[0].bitcast(I32))
         nc.sync.dma_start(d_word_table[:, EARLY:G].bitcast(I32), d_words_i32[:, EARLY:G])
@@ -94,7 +94,7 @@ def tile_picked_scorefight_none_p_kernel(
                 x_word_table[:].indirect(offs_t[:, h * (HALF // 16) : (h + 1) * (HALF // 16)]),
             )
 
-        w_raw = keep.tile([P, PACK, N], F32, name="w_raw", tag="late", align_bytes=64)
+        w_raw = keep.tile([P, PACK, N], F32, name="w_raw", tag="w_then_z", align_bytes=64)
         nc.sync.dma_start(w_raw[:], w1.rearrange("(p t) m -> p t m", t=PACK))
 
         banks = [psum.tile([P, S], F32, name="bank%d" % b) for b in range(8)]
@@ -150,7 +150,10 @@ def tile_picked_scorefight_none_p_kernel(
             out=w_words[:].bitcast(FP8X4), scales=w_scales[:], in_=w_grouped[:].rearrange("p m t -> p (m t)")
         )
 
-        z_grouped = [keep.tile([P, HALF, PACK], BF16, name="z_grouped%d" % h, align_bytes=64) for h in range(2)]
+        z_grouped = [
+            keep.tile([P, HALF, PACK], BF16, name="z_grouped0", tag="w_then_z", align_bytes=64),
+            keep.tile([P, HALF, PACK], BF16, name="z_grouped1", align_bytes=64),
+        ]
         for t in ORDER:
             last = t == ORDER[-1]
             wa, wb = wins[t]

@@ -116,26 +116,41 @@ def tile_picked_scorefight_none_p_kernel(
             cols = slice(h * HALF, (h + 1) * HALF)
             score(ORDER[0], banks[h], cols)
             nc.scalar.copy(scores[ORDER[0]][:, cols], banks[h][:, cols])
-        for n, t in enumerate(ORDER[1:]):
+        first, second, third, last = ORDER
+        for n, t in enumerate((third, second, last)):
             score(t, banks[n + 2], slice(0, S))
-            nc.scalar.copy(scores[t][:], banks[n + 2][:])
+        nc.scalar.copy(scores[third][:, 0 : S - QUARTER], banks[2][:, 0 : S - QUARTER])
+        nc.scalar.copy(scores[second][:], banks[3][:])
+        nc.scalar.copy(scores[third][:, S - QUARTER : S], banks[2][:, S - QUARTER : S])
+        nc.scalar.copy(scores[last][:], banks[4][:])
 
-        leads, wins = {}, {}
+        a_scores = [keep.tile([P, V], F32, name="a%d" % t) for t in range(PACK)]
+        leads = [keep.tile([P, V], F32, name="lead%d" % t) for t in range(PACK)]
 
-        def fight(t, tag):
-            wa = keep.tile([P, V], F32, name="wa%d" % t, tag=tag)
-            wb = keep.tile([P, V], F32, name="wb%d" % t)
-            nc.scalar.activation(wa[:], leads[t][:], ACT.Relu, scale=-1.0)
-            nc.scalar.activation(wb[:], leads[t][:], ACT.Relu)
-            wins[t] = (wa, wb)
+        def fetch_a(t):
+            nc.vector.tensor_copy(a_scores[t][:], scores[t][:].indirect(la_t[:]))
 
-        for t in ORDER:
-            a = keep.tile([P, V], F32, name="a%d" % t)
-            leads[t] = keep.tile([P, V], F32, name="lead%d" % t)
-            nc.vector.tensor_copy(a[:], scores[t][:].indirect(la_t[:]))
-            nc.vector.tensor_tensor(leads[t][:], scores[t][:].indirect(lb_t[:]), a[:], ALU.subtract)
-            if t != ORDER[-1]:
-                fight(t, "wa%d" % t)
+        def fetch_lead(t):
+            nc.vector.tensor_tensor(leads[t][:], scores[t][:].indirect(lb_t[:]), a_scores[t][:], ALU.subtract)
+
+        fetch_a(first)
+        fetch_lead(first)
+        fetch_a(second)
+        fetch_a(third)
+        fetch_lead(second)
+        fetch_a(last)
+        fetch_lead(third)
+        fetch_lead(last)
+
+        wins = {}
+
+        def win(t, side, tag):
+            wins[t, side] = keep.tile([P, V], F32, name="win%d_%d" % (t, side), tag=tag)
+            nc.scalar.activation(wins[t, side][:], leads[t][:], ACT.Relu, scale=(-1.0, 1.0)[side])
+
+        early = ((first, 0), (second, 0), (first, 1), (third, 0), (second, 1), (third, 1))
+        for t, side in early:
+            win(t, side, "win%d_%d" % (t, side))
 
         w_grouped = keep.tile([P, N, PACK], BF16, name="w_grouped", align_bytes=64)
         w_words = keep.tile([P, N], U32, name="w_words", align_bytes=64)
@@ -154,24 +169,26 @@ def tile_picked_scorefight_none_p_kernel(
             keep.tile([P, HALF, PACK], BF16, name="z_grouped0", tag="w_then_z", align_bytes=64),
             keep.tile([P, HALF, PACK], BF16, name="z_grouped1", align_bytes=64),
         ]
-        for t in ORDER:
-            last = t == ORDER[-1]
-            wa, wb = wins[t]
-            placed = keep.tile([P, S], F32, name="placed%d" % t, tag="placed%d" % t)
-            nc.vector.tensor_copy(placed[:].indirect(la_t[:]), wa[:])
-            nc.vector.tensor_copy(placed[:].indirect(lb_t[:]), wb[:])
+        placed = {}
+        for t, side in early + ((last, 0), (last, 1)):
+            if side == 0:
+                placed[t] = keep.tile([P, S], F32, name="placed%d" % t, tag="placed%d" % t)
+            nc.vector.tensor_copy(placed[t][:].indirect((la_t, lb_t)[side][:]), wins[t, side][:])
+            if side == 0:
+                continue
             for h in range(2):
                 cols = slice(h * HALF, (h + 1) * HALF)
-                if last and h == 0:
+                if t == last and h == 0:
                     for u in range(2):
                         part = slice(u * QUARTER, (u + 1) * QUARTER)
                         nc.vector.tensor_scalar(
-                            z_grouped[h][:, part, t], placed[:, part], gain[:, t : t + 1], None, ALU.mult
+                            z_grouped[h][:, part, t], placed[t][:, part], gain[:, t : t + 1], None, ALU.mult
                         )
                 else:
-                    nc.scalar.activation(z_grouped[h][:, :, t], placed[:, cols], ACT.Copy, scale=gain[:, t : t + 1])
-            if t == ORDER[0]:
-                fight(ORDER[-1], "placed%d" % t)
+                    nc.scalar.activation(z_grouped[h][:, :, t], placed[t][:, cols], ACT.Copy, scale=gain[:, t : t + 1])
+            if t == first:
+                win(last, 0, "placed%d" % t)
+                win(last, 1, "win%d_1" % last)
 
         for h, parts in enumerate(([slice(0, QUARTER), slice(QUARTER, HALF)], [slice(0, HALF)])):
             z_words = keep.tile([P, HALF], U32, name="z_words%d" % h, align_bytes=64)

from contextlib import ExitStack

import concourse.mybir as mybir

K, T, S, V, N, G, H = 512, 2048, 512, 256, 512, 2048, 512
FLOPS = 2 * K * H * S + 2 * H * N * S

F32 = mybir.dt.float32
BF16 = mybir.dt.bfloat16
I32 = mybir.dt.int32
U32 = mybir.dt.uint32
U16 = mybir.dt.uint16
U8 = mybir.dt.uint8
FP8X4 = mybir.dt.float8_e4m3fn_x4
ACT = mybir.ActivationFunctionType
ALU = mybir.AluOpType

P = 128
PACK = 4
HALF = S // 2
SCORE_SCALE = 0.0625
ORDER = (2, 0, 1, 3)
EARLY = 512
QUARTER = HALF // 2


def tile_picked_scorefight_none_p_kernel(
    tc, x_words, x_scales, d_words, d_scales, gn, w1, offs, kidx, la, lb, out
):
    nc = tc.nc
    with ExitStack() as ctx:
        lists = ctx.enter_context(tc.tile_pool(name="lists", bufs=1))
        keep = ctx.enter_context(tc.tile_pool(name="keep", bufs=1))
        psum = ctx.enter_context(tc.psum_pool(name="psum", bufs=1))

        kidx_t = lists.tile([P, H // 16], U16, name="kidx_t")
        offs_t = lists.tile([P, S // 16], U16, name="offs_t")
        la_t = lists.tile([P, V // 16], U16, name="la_t")
        lb_t = lists.tile([P, V // 16], U16, name="lb_t")

        d_scale_table = keep.tile([P, G], U8, name="d_scale_table", align_bytes=64)
        x_scale_table = keep.tile([P, T], U8, name="x_scale_table", align_bytes=64)
        d_word_table = keep.tile([P, G], U32, name="d_word_table", align_bytes=64)
        x_word_table = keep.tile([P, T], U32, name="x_word_table", align_bytes=64)
        gain = keep.tile([P, PACK], F32, name="gain")
        gain_raw = keep.tile([P, PACK], F32, name="gain_raw")

        nc.vector.memset(x_scale_table[:].bitcast(I32), 0)
        nc.vector.memset(d_scale_table[:].bitcast(I32), 0)

        d_words_i32 = d_words[0].rearrange("p n t -> p (n t)").bitcast(I32)
        nc.sync.dma_start(d_word_table[:, 0:EARLY].bitcast(I32), d_words_i32[:, 0:EARLY])
        nc.sync.dma_start(offs_t[:], offs)
        nc.sync.dma_start(kidx_t[:], kidx)
        nc.sync.dma_start(x_scale_table[0:P:8, :].bitcast(I32), x_scales[0].bitcast(I32))
        nc.sync.dma_start(d_scale_table[0:P:8, :].bitcast(I32), d_scales[0].bitcast(I32))
        nc.sync.dma_start(d_word_table[:, EARLY:G].bitcast(I32), d_words_i32[:, EARLY:G])
        nc.sync.dma_start(gain_raw[:], gn.rearrange("(p t) o -> p (t o)", t=PACK))
        nc.sync.dma_start(la_t[:], la)
        nc.sync.dma_start(lb_t[:], lb)
        nc.sync.dma_start(x_word_table[:].bitcast(I32), x_words[0].rearrange("p n t -> p (n t)").bitcast(I32))
        nc.scalar.activation(gain[:], gain_raw[:], ACT.Copy, scale=SCORE_SCALE)

        d_scales_picked = keep.tile([P, H], U8, name="d_scales_picked", align_bytes=64)
        x_scales_picked = keep.tile([P, S], U8, name="x_scales_picked", align_bytes=64)
        key_scales = keep.tile([P, H], U8, name="key_scales", align_bytes=64)
        query_scales = keep.tile([P, S], U8, name="query_scales", align_bytes=64)
        nc.vector.memset(query_scales[:].bitcast(I32), 0)
        nc.vector.tensor_copy(x_scales_picked[:], x_scale_table[:].indirect(offs_t[:]))
        for c in range(4):
            nc.sync.dma_start(
                query_scales[c:P:32, :].bitcast(I32), x_scales_picked[8 * c : P : 32, :].bitcast(I32)
            )
        nc.vector.tensor_copy(d_scales_picked[:], d_scale_table[:].indirect(kidx_t[:]))
        nc.vector.tensor_copy(
            key_scales[:].rearrange("p (t m) -> p t m", t=PACK),
            d_scales_picked[:].rearrange("p (m t) -> p t m", t=PACK),
        )
        for c in range(1, 4):
            nc.sync.dma_start(key_scales[c:P:32, :].bitcast(I32), key_scales[8 * c : P : 32, :].bitcast(I32))

        d_words_picked = keep.tile([P, H], U32, name="d_words_picked", align_bytes=64)
        key_words = keep.tile([P, H], U32, name="key_words", align_bytes=64)
        nc.vector.tensor_copy(d_words_picked[:], d_word_table[:].indirect(kidx_t[:]))
        nc.vector.tensor_copy(
            key_words[:].bitcast(I32).rearrange("p (t c i) -> p c t i", t=PACK, i=4),
            d_words_picked[:].bitcast(I32).rearrange("p (c i t) -> p c t i", t=PACK, i=4),
        )

        query_words = keep.tile([P, S], U32, name="query_words", align_bytes=64)
        for h in range(2):
            nc.vector.tensor_copy(
                query_words[:, h * HALF : (h + 1) * HALF],
                x_word_table[:].indirect(offs_t[:, h * (HALF // 16) : (h + 1) * (HALF // 16)]),
            )

        w_raw = keep.tile([P, PACK, N], F32, name="w_raw", tag="w_then_z", align_bytes=64)
        nc.sync.dma_start(w_raw[:], w1.rearrange("(p t) m -> p t m", t=PACK))

        banks = [psum.tile([P, S], F32, name="bank%d" % b) for b in range(8)]

        def score(t, bank, cols):
            keys = slice(t * P, (t + 1) * P)
            nc.tensor.matmul_mx(
                out=bank[:, cols],
                lhsT=key_words[:, keys].bitcast(FP8X4),
                lhsT_scale=key_scales[:, keys],
                rhs=query_words[:, cols].bitcast(FP8X4),
                rhs_scale=query_scales[:, cols],
                start=True,
                stop=True,
            )

        scores = [keep.tile([P, S], F32, name="scores%d" % t) for t in range(PACK)]
        for h in range(2):
            cols = slice(h * HALF, (h + 1) * HALF)
            score(ORDER[0], banks[h], cols)
            nc.scalar.copy(scores[ORDER[0]][:, cols], banks[h][:, cols])
        first, second, third, last = ORDER
        for n, t in enumerate((third, second, last)):
            score(t, banks[n + 2], slice(0, S))
        nc.scalar.copy(scores[third][:, 0 : S - QUARTER], banks[2][:, 0 : S - QUARTER])
        nc.scalar.copy(scores[second][:], banks[3][:])
        nc.scalar.copy(scores[third][:, S - QUARTER : S], banks[2][:, S - QUARTER : S])
        nc.scalar.copy(scores[last][:], banks[4][:])

        a_scores = [keep.tile([P, V], F32, name="a%d" % t) for t in range(PACK)]
        leads = [keep.tile([P, V], F32, name="lead%d" % t) for t in range(PACK)]

        def fetch_a(t):
            nc.vector.tensor_copy(a_scores[t][:], scores[t][:].indirect(la_t[:]))

        def fetch_lead(t):
            nc.vector.tensor_tensor(leads[t][:], scores[t][:].indirect(lb_t[:]), a_scores[t][:], ALU.subtract)

        fetch_a(first)
        fetch_lead(first)
        fetch_a(second)
        fetch_a(third)
        fetch_lead(second)
        fetch_a(last)
        fetch_lead(third)
        fetch_lead(last)

        wins = {}

        def win(t, side, tag):
            wins[t, side] = keep.tile([P, V], F32, name="win%d_%d" % (t, side), tag=tag)
            nc.scalar.activation(wins[t, side][:], leads[t][:], ACT.Relu, scale=(-1.0, 1.0)[side])

        early = ((first, 0), (second, 0), (first, 1), (third, 0), (second, 1), (third, 1))
        for t, side in early:
            win(t, side, "win%d_%d" % (t, side))

        w_grouped = keep.tile([P, N, PACK], BF16, name="w_grouped", align_bytes=64)
        w_words = keep.tile([P, N], U32, name="w_words", align_bytes=64)
        w_scales = keep.tile([P, N], U8, name="w_scales", align_bytes=64)
        for mt in range(N // P):
            cols = slice(mt * P, (mt + 1) * P)
            nc.scalar.copy(
                w_grouped[:, cols, :].rearrange("p (c i) t -> p c t i", i=4),
                w_raw[:, :, cols].rearrange("p t (c i) -> p c t i", i=4),
            )
        nc.vector.quantize_mx(
            out=w_words[:].bitcast(FP8X4), scales=w_scales[:], in_=w_grouped[:].rearrange("p m t -> p (m t)")
        )

        z_grouped = [
            keep.tile([P, HALF, PACK], BF16, name="z_grouped0", tag="w_then_z", align_bytes=64),
            keep.tile([P, HALF, PACK], BF16, name="z_grouped1", align_bytes=64),
        ]
        placed = {}
        for t, side in early + ((last, 0), (last, 1)):
            if side == 0:
                placed[t] = keep.tile([P, S], F32, name="placed%d" % t, tag="placed%d" % t)
            nc.vector.tensor_copy(placed[t][:].indirect((la_t, lb_t)[side][:]), wins[t, side][:])
            if side == 0:
                continue
            for h in range(2):
                cols = slice(h * HALF, (h + 1) * HALF)
                if t == last and h == 0:
                    for u in range(2):
                        part = slice(u * QUARTER, (u + 1) * QUARTER)
                        nc.vector.tensor_scalar(
                            z_grouped[h][:, part, t], placed[t][:, part], gain[:, t : t + 1], None, ALU.mult
                        )
                else:
                    nc.scalar.activation(z_grouped[h][:, :, t], placed[t][:, cols], ACT.Copy, scale=gain[:, t : t + 1])
            if t == first:
                win(last, 0, "placed%d" % t)
                win(last, 1, "win%d_1" % last)

        for h, parts in enumerate(([slice(0, QUARTER), slice(QUARTER, HALF)], [slice(0, HALF)])):
            z_words = keep.tile([P, HALF], U32, name="z_words%d" % h, align_bytes=64)
            z_scales = keep.tile([P, HALF], U8, name="z_scales%d" % h, align_bytes=64)
            for part in parts:
                nc.vector.quantize_mx(
                    out=z_words[:, part].bitcast(FP8X4),
                    scales=z_scales[:, part],
                    in_=z_grouped[h][:, part, :].rearrange("p j t -> p (j t)"),
                )
            for mt in range(N // P):
                bank = banks[4 * h + mt]
                rows = slice(mt * P, (mt + 1) * P)
                for part in parts:
                    nc.tensor.matmul_mx(
                        out=bank[:, part],
                        lhsT=w_words[:, rows].bitcast(FP8X4),
                        lhsT_scale=w_scales[:, rows],
                        rhs=z_words[:, part].bitcast(FP8X4),
                        rhs_scale=z_scales[:, part],
                        start=True,
                        stop=True,
                    )
                result = keep.tile([P, HALF], F32, name="result%d_%d" % (h, mt))
                if mt % 2 == 0:
                    nc.scalar.copy(result[:], bank[:, 0:HALF])
                else:
                    nc.vector.tensor_copy(result[:], bank[:, 0:HALF])
                nc.sync.dma_start(out[rows, h * HALF : (h + 1) * HALF], result[:])
